import numpy as np
import ml_dtypes


def mxq(x, axis, fmt="e4m3"):
    dtype, down = {"e4m3": (ml_dtypes.float8_e4m3fn, 7), "e5m2": (ml_dtypes.float8_e5m2, 14)}[fmt]
    v = np.moveaxis(np.asarray(x, np.float32).astype(ml_dtypes.bfloat16).astype(np.float64), axis, -1)
    blocks = v.reshape(v.shape[:-1] + (-1, 32))
    amax = np.abs(blocks).max(-1, keepdims=True)
    byte = np.maximum(np.where(amax > 0, np.frexp(amax)[1] - 1 + 127, 0) - down, 1)
    scale = np.exp2(byte - 127.0)
    codes = (blocks / scale).astype(np.float32).astype(dtype).astype(np.float64)
    return np.moveaxis((codes * scale).reshape(v.shape), -1, axis)


WIDE = False


def mx_kscale(k):
    if not WIDE:
        return np.ones(k)
    levels = np.array([30, -30])
    if k % 512:
        return np.exp2(np.random.permutation(np.resize(levels, k // 32))).repeat(32)
    a = np.empty((k // 512, 16))
    for p in range(k // 512):
        a[p, :8] = np.random.permutation(np.resize(levels, 8))
        for g in range(8):
            far = levels[np.abs(levels - a[p, g]) >= 10]
            a[p, g + 8] = far[np.random.randint(len(far))]
    return np.exp2(a.ravel()).repeat(32)


def f64(x):
    return np.asarray(x).astype(np.float64)


def striped(idx):
    return np.tile(np.asarray(idx).reshape(-1, 16).T, (8, 1)).astype(np.uint16)


def unstriped(offs):
    return offs[:16].T.reshape(-1).astype(np.int64)


E2M1 = np.array([0.0, 0.5, 1.0, 1.5, 2.0, 3.0, 4.0, 6.0, -0.0, -0.5, -1.0, -1.5, -2.0, -3.0, -4.0, -6.0])


def pack_weight(w, fmt):
    k, n = w.shape
    w = f64(np.asarray(w, np.float32).astype(ml_dtypes.bfloat16)).reshape(k // 32, 32, n)
    amax = np.abs(w).max(1)
    if fmt in ("e4m3", "e5m2"):
        byte = np.frexp(amax)[1] - 1 + 127 - (7 if fmt == "e4m3" else 14)
    else:
        mant, ex = np.frexp(amax / 6.0)
        byte = np.where(mant > 0.5, ex, ex - 1) + 127
    byte = np.clip(np.where(amax > 0, byte, 1), 1, 254)
    scaled = (w * np.exp2(127.0 - byte)[:, None, :]).reshape(k, n).astype(np.float32)
    by_word = np.ascontiguousarray(scaled.reshape(k // 512, 128, 4, n).transpose(0, 1, 3, 2))
    if fmt in ("e4m3", "e5m2"):
        words = by_word.astype(ml_dtypes.float8_e4m3fn if fmt == "e4m3" else ml_dtypes.float8_e5m2).view(np.uint8)
    else:
        c = by_word.astype(ml_dtypes.float4_e2m1fn).view(np.uint8) & 0xF
        words = (c[..., 0::2] | (c[..., 1::2] << 4)).reshape(k // 512, 128, 2 * n)
    return np.ascontiguousarray(words), np.ascontiguousarray(byte.astype(np.uint8).reshape(k // 512, 16, n))


def unpack_weight(words, scales, fmt):
    g, _, n = scales.shape
    words = np.ascontiguousarray(words).reshape(g, 128, n, -1)
    if fmt in ("e4m3", "e5m2"):
        vals = words.view(ml_dtypes.float8_e4m3fn if fmt == "e4m3" else ml_dtypes.float8_e5m2).astype(np.float64)
    else:
        nib = np.empty((g, 128, n, 4), np.uint8)
        nib[..., 0::2] = words & 0xF
        nib[..., 1::2] = words >> 4
        vals = E2M1[nib]
    vals = vals * np.repeat(np.exp2(scales.astype(np.float64) - 127.0), 8, axis=1)[..., None]
    return vals.transpose(0, 1, 3, 2).reshape(g * 512, n)


K, J, N, T, B = 256, 1024, 256, 2048, 128


def setup_inputs():
    n = np.random.standard_normal
    idx = np.random.permutation(T)[:J]
    fj = mx_kscale(J)
    gjp = pack_weight(n((J, N)) * np.exp(0.5 * n((J, 1))) / fj[:, None], "e5m2")
    return {
        "xf": (n((K, T))).astype(np.float32),
        "ra": (np.random.uniform(0.5, 1.5, (1, J)) * fj).astype(np.float32),
        "gj_words": gjp[0],
        "gj_scales": gjp[1],
        "old": (12.0 * n((K, N))).astype(np.float32),
        "offs": striped(idx),
    }


def reference(xf, ra, gj_words, gj_scales, old, offs):
    idx = unstriped(offs)
    gju = unpack_weight(gj_words, gj_scales, "e5m2")
    xg = f64(xf)[:, idx]
    g1 = xg.reshape(K, B, J // B).mean(axis=2)
    g2 = np.repeat(g1, J // B, axis=1)
    us = (xg - g2) * f64(ra)
    uj = us.T
    ujq = mxq(uj, 0, "e4m3")
    w = ujq.T @ gju
    y = 0.04 * np.maximum(w, f64(old))
    return y

@@ -1,0 +1,130 @@
+from contextlib import ExitStack
+
+import concourse.mybir as mybir
+from concourse.masks import make_identity
+
+K, J, N, T = 256, 1024, 256, 2048
+P = 128
+PACK = 4
+J_PASS = P * PACK
+GROUP = 8
+KEEP = 0.04
+FLOPS = 2 * K * J * N
+
+F32 = mybir.dt.float32
+BF16 = mybir.dt.bfloat16
+I32 = mybir.dt.int32
+U32 = mybir.dt.uint32
+U16 = mybir.dt.uint16
+U8 = mybir.dt.uint8
+E4M3X4 = mybir.dt.float8_e4m3fn_x4
+E5M2X4 = mybir.dt.float8_e5m2_x4
+ALU = mybir.AluOpType
+COPY = mybir.ActivationFunctionType.Copy
+
+
+def tile_list_moment_centred_stored_larger_kernel(tc, xf, ra, gj_words, gj_scales, old, offs, out):
+    nc = tc.nc
+    k_tiles = K // P
+    passes = J // J_PASS
+    groups = J_PASS // GROUP
+    cols = J_PASS // 16
+
+    with ExitStack() as ctx:
+        sb = ctx.enter_context(tc.tile_pool(name="sb", bufs=1))
+        ps = ctx.enter_context(tc.psum_pool(name="ps", bufs=1))
+
+        offsets = sb.tile([P, J // 16], U16, name="offsets")
+        nc.sync.dma_start(offsets[:], offs)
+        x_rows = [sb.tile([P, T], F32, name=f"x_rows{c}") for c in range(k_tiles)]
+        ra_p = sb.tile([P, passes, PACK], F32, name="ra_p")
+        nc.scalar.dma_start(out=ra_p[:], in_=ra.rearrange("o (z p t) -> p (o z) t", z=passes, t=PACK))
+        nc.sync.dma_start(out=x_rows[0][:], in_=xf[0:P, :])
+        nc.sync.dma_start(out=x_rows[1][:], in_=xf[P : 2 * P, :])
+        ra_kt = sb.tile([P, passes, P, PACK], F32, name="ra_kt")
+        nc.scalar.activation(ra_kt[:], ra_p[:].unsqueeze(2).to_broadcast([P, passes, P, PACK]), COPY)
+
+        ident = sb.tile([P, P], F32, name="ident")
+        make_identity(nc, ident[:])
+        g_scales = sb.tile([P, passes, N], U8, name="g_scales", align_bytes=64)
+        nc.gpsimd.memset(g_scales[:].bitcast(I32), 0)
+
+        g_words = sb.tile([P, passes, N], U32, name="g_words", align_bytes=64)
+        nc.sync.dma_start(out=g_words[:].bitcast(I32), in_=gj_words.rearrange("z p n t -> p z (n t)").bitcast(I32))
+        for q in range(4):
+            nc.sync.dma_start(
+                out=g_scales[32 * q : 32 * q + 4].bitcast(I32),
+                in_=gj_scales[:, 4 * q : 4 * q + 4, :].rearrange("z r n -> r z n").bitcast(I32),
+            )
+        old_sb = sb.tile([P, k_tiles, N], F32, name="old_sb")
+        nc.sync.dma_start(out=old_sb[:], in_=old.rearrange("(c p) n -> p c n", p=P))
+
+        chunks = [(c, z) for c in range(k_tiles) for z in range(passes)]
+        picked, centred, codes, scales = {}, {}, {}, {}
+
+        def gather(i):
+            c, z = chunks[i]
+            picked[i] = sb.tile([P, J_PASS], F32, name=f"picked{i}")
+            lo = z * cols
+            if i == 0:
+                half = cols // 2
+                nc.vector.tensor_copy(picked[i][:, 0 : J_PASS // 2], x_rows[c][:].indirect(offsets[:, lo : lo + half]))
+                nc.scalar.activation(picked[i][:, J_PASS // 2 :], x_rows[c][:].indirect(offsets[:, lo + half : lo + cols]), COPY)
+            else:
+                nc.scalar.activation(picked[i][:], x_rows[c][:].indirect(offsets[:, lo : lo + cols]), COPY)
+
+        def centre(i):
+            sums = sb.tile([P, groups], F32, name=f"sums{i}")
+            nc.vector.tensor_reduce(sums[:], picked[i][:].rearrange("p (b g) -> p b g", g=GROUP), mybir.AxisListType.X, ALU.add)
+            neg = sb.tile([P, groups, 2], F32, name=f"neg{i}")
+            nc.gpsimd.tensor_scalar(neg[:], sums[:].unsqueeze(2).to_broadcast([P, groups, 2]), -1.0 / GROUP, 0.0, ALU.mult, ALU.add)
+            centred[i] = ps.tile([P, PACK, P], F32, name=f"centred{i}")
+            for t in range(PACK):
+                nc.tensor.matmul(centred[i][:, t, :], picked[i][:, t:J_PASS:PACK], ident[:], start=(t == 0), stop=False, is_transpose=True)
+            for t in range(PACK):
+                nc.tensor.matmul(centred[i][:, t, :], neg[:].rearrange("p b e -> p (b e)"), ident[:], start=False, stop=(t == PACK - 1), is_transpose=True)
+
+        def weigh(i):
+            c, z = chunks[i]
+            u = sb.tile([P, P, PACK], BF16, name=f"u{i}", align_bytes=64)
+            nc.vector.tensor_tensor(u[:], centred[i][:].rearrange("p t k -> p k t"), ra_kt[:, z], ALU.mult)
+            return u
+
+        def quantise(i, u):
+            codes[i] = sb.tile([P, P], U32, name=f"codes{i}", align_bytes=64)
+            scales[i] = sb.tile([P, P], U8, name=f"scales{i}", align_bytes=64)
+            nc.vector.quantize_mx(out=codes[i][:].bitcast(E4M3X4), scales=scales[i][:], in_=u[:].rearrange("p k t -> p (k t)"))
+
+        old_kept = sb.tile([P, k_tiles, N], F32, name="old_kept")
+
+        def finish(c):
+            acc = ps.tile([P, N], F32, name=f"acc{c}")
+            for z in range(passes):
+                i = c * passes + z
+                nc.tensor.matmul_mx(
+                    out=acc[:], lhsT=codes[i][:].bitcast(E4M3X4), lhsT_scale=scales[i][:],
+                    rhs=g_words[:, z, :].bitcast(E5M2X4), rhs_scale=g_scales[:, z, :],
+                    start=(z == 0), stop=(z == passes - 1),
+                )
+            res = sb.tile([P, N], F32, name=f"res{c}")
+            nc.vector.scalar_tensor_tensor(res[:], acc[:], KEEP, old_kept[:, c, :], ALU.mult, ALU.max)
+            nc.sync.dma_start(out=out[c * P : (c + 1) * P, :], in_=res[:])
+
+        for i in range(len(chunks)):
+            gather(i)
+        nc.scalar.activation(old_kept[:], old_sb[:], COPY, scale=KEEP)
+        us = {}
+        centre(0)
+        centre(1)
+        us[0] = weigh(0)
+        centre(2)
+        quantise(0, us[0])
+        us[1] = weigh(1)
+        centre(3)
+        quantise(1, us[1])
+        us[2] = weigh(2)
+        finish(0)
+        quantise(2, us[2])
+        us[3] = weigh(3)
+        quantise(3, us[3])
+        finish(1)

@@ -35,14 +35,14 @@ def tile_list_moment_centred_stored_larger_kernel(tc, xf, ra, gj_words, gj_scale
         ps = ctx.enter_context(tc.psum_pool(name="ps", bufs=1))
 
         offsets = sb.tile([P, J // 16], U16, name="offsets")
-        nc.sync.dma_start(offsets[:], offs)
         x_rows = [sb.tile([P, T], F32, name=f"x_rows{c}") for c in range(k_tiles)]
         ra_p = sb.tile([P, passes, PACK], F32, name="ra_p")
         nc.scalar.dma_start(out=ra_p[:], in_=ra.rearrange("o (z p t) -> p (o z) t", z=passes, t=PACK))
         nc.sync.dma_start(out=x_rows[0][:], in_=xf[0:P, :])
+        nc.sync.dma_start(offsets[:], offs)
         nc.sync.dma_start(out=x_rows[1][:], in_=xf[P : 2 * P, :])
-        ra_kt = sb.tile([P, passes, P, PACK], F32, name="ra_kt")
-        nc.scalar.activation(ra_kt[:], ra_p[:].unsqueeze(2).to_broadcast([P, passes, P, PACK]), COPY)
+        ra_first = sb.tile([P, 1, PACK], F32, name="ra_first", tag="sums3")
+        nc.scalar.activation(ra_first[:], ra_p[:, 0:1, :], COPY)
 
         ident = sb.tile([P, P], F32, name="ident")
         make_identity(nc, ident[:])
@@ -60,71 +60,98 @@ def tile_list_moment_centred_stored_larger_kernel(tc, xf, ra, gj_words, gj_scale
         nc.sync.dma_start(out=old_sb[:], in_=old.rearrange("(c p) n -> p c n", p=P))
 
         chunks = [(c, z) for c in range(k_tiles) for z in range(passes)]
-        picked, centred, codes, scales = {}, {}, {}, {}
+        picked, planes, centred, codes, scales = {}, {}, {}, {}, {}
 
         def gather(i):
             c, z = chunks[i]
             picked[i] = sb.tile([P, J_PASS], F32, name=f"picked{i}")
             lo = z * cols
-            if i == 0:
+            if i < len(chunks) - 1:
                 half = cols // 2
                 nc.vector.tensor_copy(picked[i][:, 0 : J_PASS // 2], x_rows[c][:].indirect(offsets[:, lo : lo + half]))
                 nc.scalar.activation(picked[i][:, J_PASS // 2 :], x_rows[c][:].indirect(offsets[:, lo + half : lo + cols]), COPY)
             else:
                 nc.scalar.activation(picked[i][:], x_rows[c][:].indirect(offsets[:, lo : lo + cols]), COPY)
 
+        def part(i):
+            if i % 2 == 0:
+                planes[i] = [picked[i][:, t:J_PASS:PACK] for t in range(PACK)]
+                return
+            parted = sb.tile([P, PACK, P], F32, name=f"parted{i}")
+            nc.scalar.copy(
+                parted[:].rearrange("p t (a b) -> p a t b", b=4),
+                picked[i][:].rearrange("p (a b t) -> p a t b", b=4, t=PACK),
+            )
+            planes[i] = [parted[:, t, :] for t in range(PACK)]
+
         def centre(i):
-            sums = sb.tile([P, groups], F32, name=f"sums{i}")
+            sums = sb.tile([P, groups], F32, name=f"sums{i}", tag=f"sums{i}")
             nc.vector.tensor_reduce(sums[:], picked[i][:].rearrange("p (b g) -> p b g", g=GROUP), mybir.AxisListType.X, ALU.add)
             neg = sb.tile([P, groups, 2], F32, name=f"neg{i}")
-            nc.gpsimd.tensor_scalar(neg[:], sums[:].unsqueeze(2).to_broadcast([P, groups, 2]), -1.0 / GROUP, 0.0, ALU.mult, ALU.add)
-            centred[i] = ps.tile([P, PACK, P], F32, name=f"centred{i}")
+            twice = sums[:].unsqueeze(2).to_broadcast([P, groups, 2])
+            if i == len(chunks) - 1:
+                nc.scalar.activation(neg[:], twice, COPY, scale=-1.0 / GROUP)
+            else:
+                nc.gpsimd.tensor_scalar(neg[:], twice, -1.0 / GROUP, 0.0, ALU.mult, ALU.add)
+            centred[i] = ps.tile([P, PACK, P], F32, name=f"centred{i}", tag=f"bank{i}")
             for t in range(PACK):
-                nc.tensor.matmul(centred[i][:, t, :], picked[i][:, t:J_PASS:PACK], ident[:], start=(t == 0), stop=False, is_transpose=True)
+                nc.tensor.matmul(centred[i][:, t, :], planes[i][t], ident[:], start=(t == 0), stop=False, is_transpose=True)
             for t in range(PACK):
                 nc.tensor.matmul(centred[i][:, t, :], neg[:].rearrange("p b e -> p (b e)"), ident[:], start=False, stop=(t == PACK - 1), is_transpose=True)
 
         def weigh(i):
             c, z = chunks[i]
-            u = sb.tile([P, P, PACK], BF16, name=f"u{i}", align_bytes=64)
-            nc.vector.tensor_tensor(u[:], centred[i][:].rearrange("p t k -> p k t"), ra_kt[:, z], ALU.mult)
-            return u
+            weights = ra_first[:] if i == 0 else ra_p[:, z : z + 1, :]
+            nc.vector.tensor_tensor(u[i], centred[i][:].rearrange("p t k -> p k t"), weights.to_broadcast([P, P, PACK]), ALU.mult)
 
-        def quantise(i, u):
-            codes[i] = sb.tile([P, P], U32, name=f"codes{i}", align_bytes=64)
-            scales[i] = sb.tile([P, P], U8, name=f"scales{i}", align_bytes=64)
-            nc.vector.quantize_mx(out=codes[i][:].bitcast(E4M3X4), scales=scales[i][:], in_=u[:].rearrange("p k t -> p (k t)"))
+        def quantise(first, rows):
+            n = rows.shape[1]
+            words = sb.tile([P, n * P], U32, name=f"codes{first}", align_bytes=64)
+            plane = sb.tile([P, n * P], U8, name=f"scales{first}", align_bytes=64)
+            nc.vector.quantize_mx(out=words[:].bitcast(E4M3X4), scales=plane[:], in_=rows[:].rearrange("p z k t -> p (z k t)"))
+            for z in range(n):
+                codes[first + z] = words[:, z * P : (z + 1) * P]
+                scales[first + z] = plane[:, z * P : (z + 1) * P]
 
-        old_kept = sb.tile([P, k_tiles, N], F32, name="old_kept")
 
-        def finish(c):
-            acc = ps.tile([P, N], F32, name=f"acc{c}")
+        accs = {}
+
+        def multiply(c):
+            accs[c] = ps.tile([P, N], F32, name=f"acc{c}", tag=f"bank{2 if c == 0 else 0}")
             for z in range(passes):
                 i = c * passes + z
                 nc.tensor.matmul_mx(
-                    out=acc[:], lhsT=codes[i][:].bitcast(E4M3X4), lhsT_scale=scales[i][:],
+                    out=accs[c][:], lhsT=codes[i].bitcast(E4M3X4), lhsT_scale=scales[i],
                     rhs=g_words[:, z, :].bitcast(E5M2X4), rhs_scale=g_scales[:, z, :],
                     start=(z == 0), stop=(z == passes - 1),
                 )
-            res = sb.tile([P, N], F32, name=f"res{c}")
-            nc.vector.scalar_tensor_tensor(res[:], acc[:], KEEP, old_kept[:, c, :], ALU.mult, ALU.max)
+
+        def finish(c):
+            res = sb.tile([P, N], F32, name=f"res{c}", tag=f"u{3 - c}", align_bytes=64)
+            nc.vector.scalar_tensor_tensor(res[:], accs[c][:], KEEP, old_kept[:, c, :], ALU.mult, ALU.max)
             nc.sync.dma_start(out=out[c * P : (c + 1) * P, :], in_=res[:])
 
         for i in range(len(chunks)):
             gather(i)
-        nc.scalar.activation(old_kept[:], old_sb[:], COPY, scale=KEEP)
-        us = {}
+            part(i)
+        u01 = sb.tile([P, 2, P, PACK], BF16, name="u01", align_bytes=64)
+        u2 = sb.tile([P, 1, P, PACK], BF16, name="u2", tag="u2", align_bytes=64)
+        u3 = sb.tile([P, 1, P, PACK], BF16, name="u3", tag="u3", align_bytes=64)
+        u = [u01[:, 0], u01[:, 1], u2[:, 0], u3[:, 0]]
         centre(0)
         centre(1)
-        us[0] = weigh(0)
         centre(2)
-        quantise(0, us[0])
-        us[1] = weigh(1)
+        weigh(0)
         centre(3)
-        quantise(1, us[1])
-        us[2] = weigh(2)
+        old_kept = sb.tile([P, k_tiles, N], F32, name="old_kept", tag="sums3")
+        nc.scalar.activation(old_kept[:], old_sb[:], COPY, scale=KEEP)
+        weigh(1)
+        weigh(2)
+        quantise(0, u01)
+        weigh(3)
+        quantise(2, u2)
+        quantise(3, u3)
+        multiply(0)
+        multiply(1)
         finish(0)
-        quantise(2, us[2])
-        us[3] = weigh(3)
-        quantise(3, us[3])
         finish(1)

@@ -74,15 +74,15 @@ def tile_list_moment_centred_stored_larger_kernel(tc, xf, ra, gj_words, gj_scale
                 nc.scalar.activation(picked[i][:], x_rows[c][:].indirect(offsets[:, lo : lo + cols]), COPY)
 
         def part(i):
-            if i % 2 == 0:
-                planes[i] = [picked[i][:, t:J_PASS:PACK] for t in range(PACK)]
-                return
-            parted = sb.tile([P, PACK, P], F32, name=f"parted{i}")
-            nc.scalar.copy(
-                parted[:].rearrange("p t (a b) -> p a t b", b=4),
-                picked[i][:].rearrange("p (a b t) -> p a t b", b=4, t=PACK),
-            )
-            planes[i] = [parted[:, t, :] for t in range(PACK)]
+            direct = [4, 1, 2, 0][i]
+            planes[i] = [picked[i][:, t:J_PASS:PACK] for t in range(direct)]
+            if direct < PACK:
+                parted = sb.tile([P, PACK - direct, P], F32, name=f"parted{i}")
+                nc.scalar.copy(
+                    parted[:].rearrange("p t (a b) -> p a t b", b=4),
+                    picked[i][:].rearrange("p (a b t) -> p a t b", b=4, t=PACK)[:, :, direct:, :],
+                )
+                planes[i].extend(parted[:, t, :] for t in range(PACK - direct))
 
         def centre(i):
             sums = sb.tile([P, groups], F32, name=f"sums{i}", tag=f"sums{i}")
@@ -148,8 +148,8 @@ def tile_list_moment_centred_stored_larger_kernel(tc, xf, ra, gj_words, gj_scale
         weigh(1)
         weigh(2)
         quantise(0, u01)
-        weigh(3)
         quantise(2, u2)
+        weigh(3)
         quantise(3, u3)
         multiply(0)
         multiply(1)

from contextlib import ExitStack

import concourse.mybir as mybir
from concourse.masks import make_identity

K, J, N, T = 256, 1024, 256, 2048
P = 128
PACK = 4
J_PASS = P * PACK
GROUP = 8
KEEP = 0.04
FLOPS = 2 * K * J * N

F32 = mybir.dt.float32
BF16 = mybir.dt.bfloat16
I32 = mybir.dt.int32
U32 = mybir.dt.uint32
U16 = mybir.dt.uint16
U8 = mybir.dt.uint8
E4M3X4 = mybir.dt.float8_e4m3fn_x4
E5M2X4 = mybir.dt.float8_e5m2_x4
ALU = mybir.AluOpType
COPY = mybir.ActivationFunctionType.Copy


def tile_list_moment_centred_stored_larger_kernel(tc, xf, ra, gj_words, gj_scales, old, offs, out):
    nc = tc.nc
    k_tiles = K // P
    passes = J // J_PASS
    groups = J_PASS // GROUP
    cols = J_PASS // 16

    with ExitStack() as ctx:
        sb = ctx.enter_context(tc.tile_pool(name="sb", bufs=1))
        ps = ctx.enter_context(tc.psum_pool(name="ps", bufs=1))

        offsets = sb.tile([P, J // 16], U16, name="offsets")
        x_rows = [sb.tile([P, T], F32, name=f"x_rows{c}") for c in range(k_tiles)]
        ra_p = sb.tile([P, passes, PACK], F32, name="ra_p")
        nc.scalar.dma_start(out=ra_p[:], in_=ra.rearrange("o (z p t) -> p (o z) t", z=passes, t=PACK))
        nc.sync.dma_start(out=x_rows[0][:], in_=xf[0:P, :])
        nc.sync.dma_start(offsets[:], offs)
        nc.sync.dma_start(out=x_rows[1][:], in_=xf[P : 2 * P, :])
        ra_first = sb.tile([P, 1, PACK], F32, name="ra_first", tag="sums3")
        nc.scalar.activation(ra_first[:], ra_p[:, 0:1, :], COPY)

        ident = sb.tile([P, P], F32, name="ident")
        make_identity(nc, ident[:])
        g_scales = sb.tile([P, passes, N], U8, name="g_scales", align_bytes=64)
        nc.gpsimd.memset(g_scales[:].bitcast(I32), 0)

        g_words = sb.tile([P, passes, N], U32, name="g_words", align_bytes=64)
        nc.sync.dma_start(out=g_words[:].bitcast(I32), in_=gj_words.rearrange("z p n t -> p z (n t)").bitcast(I32))
        for q in range(4):
            nc.sync.dma_start(
                out=g_scales[32 * q : 32 * q + 4].bitcast(I32),
                in_=gj_scales[:, 4 * q : 4 * q + 4, :].rearrange("z r n -> r z n").bitcast(I32),
            )
        old_sb = sb.tile([P, k_tiles, N], F32, name="old_sb")
        nc.sync.dma_start(out=old_sb[:], in_=old.rearrange("(c p) n -> p c n", p=P))

        chunks = [(c, z) for c in range(k_tiles) for z in range(passes)]
        picked, planes, centred, codes, scales = {}, {}, {}, {}, {}

        def gather(i):
            c, z = chunks[i]
            picked[i] = sb.tile([P, J_PASS], F32, name=f"picked{i}")
            lo = z * cols
            if i < len(chunks) - 1:
                half = cols // 2
                nc.vector.tensor_copy(picked[i][:, 0 : J_PASS // 2], x_rows[c][:].indirect(offsets[:, lo : lo + half]))
                nc.scalar.activation(picked[i][:, J_PASS // 2 :], x_rows[c][:].indirect(offsets[:, lo + half : lo + cols]), COPY)
            else:
                nc.scalar.activation(picked[i][:], x_rows[c][:].indirect(offsets[:, lo : lo + cols]), COPY)

        def part(i):
            direct = [4, 1, 2, 0][i]
            planes[i] = [picked[i][:, t:J_PASS:PACK] for t in range(direct)]
            if direct < PACK:
                parted = sb.tile([P, PACK - direct, P], F32, name=f"parted{i}")
                nc.scalar.copy(
                    parted[:].rearrange("p t (a b) -> p a t b", b=4),
                    picked[i][:].rearrange("p (a b t) -> p a t b", b=4, t=PACK)[:, :, direct:, :],
                )
                planes[i].extend(parted[:, t, :] for t in range(PACK - direct))

        def centre(i):
            sums = sb.tile([P, groups], F32, name=f"sums{i}", tag=f"sums{i}")
            nc.vector.tensor_reduce(sums[:], picked[i][:].rearrange("p (b g) -> p b g", g=GROUP), mybir.AxisListType.X, ALU.add)
            neg = sb.tile([P, groups, 2], F32, name=f"neg{i}")
            twice = sums[:].unsqueeze(2).to_broadcast([P, groups, 2])
            if i == len(chunks) - 1:
                nc.scalar.activation(neg[:], twice, COPY, scale=-1.0 / GROUP)
            else:
                nc.gpsimd.tensor_scalar(neg[:], twice, -1.0 / GROUP, 0.0, ALU.mult, ALU.add)
            centred[i] = ps.tile([P, PACK, P], F32, name=f"centred{i}", tag=f"bank{i}")
            for t in range(PACK):
                nc.tensor.matmul(centred[i][:, t, :], planes[i][t], ident[:], start=(t == 0), stop=False, is_transpose=True)
            for t in range(PACK):
                nc.tensor.matmul(centred[i][:, t, :], neg[:].rearrange("p b e -> p (b e)"), ident[:], start=False, stop=(t == PACK - 1), is_transpose=True)

        def weigh(i):
            c, z = chunks[i]
            weights = ra_first[:] if i == 0 else ra_p[:, z : z + 1, :]
            nc.vector.tensor_tensor(u[i], centred[i][:].rearrange("p t k -> p k t"), weights.to_broadcast([P, P, PACK]), ALU.mult)

        def quantise(first, rows):
            n = rows.shape[1]
            words = sb.tile([P, n * P], U32, name=f"codes{first}", align_bytes=64)
            plane = sb.tile([P, n * P], U8, name=f"scales{first}", align_bytes=64)
            nc.vector.quantize_mx(out=words[:].bitcast(E4M3X4), scales=plane[:], in_=rows[:].rearrange("p z k t -> p (z k t)"))
            for z in range(n):
                codes[first + z] = words[:, z * P : (z + 1) * P]
                scales[first + z] = plane[:, z * P : (z + 1) * P]


        accs = {}

        def multiply(c):
            accs[c] = ps.tile([P, N], F32, name=f"acc{c}", tag=f"bank{2 if c == 0 else 0}")
            for z in range(passes):
                i = c * passes + z
                nc.tensor.matmul_mx(
                    out=accs[c][:], lhsT=codes[i].bitcast(E4M3X4), lhsT_scale=scales[i],
                    rhs=g_words[:, z, :].bitcast(E5M2X4), rhs_scale=g_scales[:, z, :],
                    start=(z == 0), stop=(z == passes - 1),
                )

        def finish(c):
            res = sb.tile([P, N], F32, name=f"res{c}", tag=f"u{3 - c}", align_bytes=64)
            nc.vector.scalar_tensor_tensor(res[:], accs[c][:], KEEP, old_kept[:, c, :], ALU.mult, ALU.max)
            nc.sync.dma_start(out=out[c * P : (c + 1) * P, :], in_=res[:])

        for i in range(len(chunks)):
            gather(i)
            part(i)
        u01 = sb.tile([P, 2, P, PACK], BF16, name="u01", align_bytes=64)
        u2 = sb.tile([P, 1, P, PACK], BF16, name="u2", tag="u2", align_bytes=64)
        u3 = sb.tile([P, 1, P, PACK], BF16, name="u3", tag="u3", align_bytes=64)
        u = [u01[:, 0], u01[:, 1], u2[:, 0], u3[:, 0]]
        centre(0)
        centre(1)
        centre(2)
        weigh(0)
        centre(3)
        old_kept = sb.tile([P, k_tiles, N], F32, name="old_kept", tag="sums3")
        nc.scalar.activation(old_kept[:], old_sb[:], COPY, scale=KEEP)
        weigh(1)
        weigh(2)
        quantise(0, u01)
        quantise(2, u2)
        weigh(3)
        quantise(3, u3)
        multiply(0)
        multiply(1)
        finish(0)
        finish(1)
